import numpy as np
import ml_dtypes


def mxq(x, axis, fmt="e4m3"):
    dtype, down = {"e4m3": (ml_dtypes.float8_e4m3fn, 7), "e5m2": (ml_dtypes.float8_e5m2, 14)}[fmt]
    v = np.moveaxis(np.asarray(x, np.float32).astype(ml_dtypes.bfloat16).astype(np.float64), axis, -1)
    blocks = v.reshape(v.shape[:-1] + (-1, 32))
    amax = np.abs(blocks).max(-1, keepdims=True)
    byte = np.maximum(np.where(amax > 0, np.frexp(amax)[1] - 1 + 127, 0) - down, 1)
    scale = np.exp2(byte - 127.0)
    codes = (blocks / scale).astype(np.float32).astype(dtype).astype(np.float64)
    return np.moveaxis((codes * scale).reshape(v.shape), -1, axis)


WIDE = False


def mx_kscale(k):
    if not WIDE:
        return np.ones(k)
    levels = np.array([10, -10, 5, -5, 0])
    if k % 512:
        return np.exp2(np.random.permutation(np.resize(levels, k // 32))).repeat(32)
    a = np.empty((k // 512, 16))
    for p in range(k // 512):
        a[p, :8] = np.random.permutation(np.resize(levels, 8))
        for g in range(8):
            far = levels[np.abs(levels - a[p, g]) >= 10]
            a[p, g + 8] = far[np.random.randint(len(far))]
    return np.exp2(a.ravel()).repeat(32)


def f64(x):
    return np.asarray(x).astype(np.float64)


def striped8(idx):
    return np.concatenate([x.reshape(-1, 16).T for x in idx]).astype(np.uint16)


def runs(offs, k):
    lists = np.stack([offs[16 * r : 16 * r + 16].T.reshape(-1) for r in range(8)]).astype(np.int64)
    return lists[np.arange(k) % 512 // 64]


def pack_weight(w):
    k, n = w.shape
    w = f64(np.asarray(w, np.float32).astype(ml_dtypes.bfloat16)).reshape(k // 32, 32, n)
    amax = np.abs(w).max(1)
    byte = np.clip(np.where(amax > 0, np.frexp(amax)[1] - 1 + 127 - 7, 1), 1, 254)
    scaled = (w * np.exp2(127.0 - byte)[:, None, :]).reshape(k, n).astype(np.float32)
    words = np.ascontiguousarray(scaled.reshape(k // 512, 128, 4, n).transpose(0, 1, 3, 2)).astype(ml_dtypes.float8_e4m3fn).view(np.uint8)
    return words, np.ascontiguousarray(byte.astype(np.uint8).reshape(k // 512, 16, n))


def unpack_weight(words, scales):
    g, p, n, _ = words.shape
    vals = np.ascontiguousarray(words).view(ml_dtypes.float8_e4m3fn).astype(np.float64) * np.repeat(np.exp2(scales.astype(np.float64) - 127.0), 8, axis=1)[..., None]
    return vals.transpose(0, 1, 3, 2).reshape(g * 512, n)

def planes(y):
    n, m = y.shape
    v = y.astype(np.float32).astype(ml_dtypes.bfloat16).astype(np.float64).reshape(n // 32, 32, m)
    top = np.abs(v).max(1)
    byte = np.clip(np.where(top > 0, np.frexp(top)[1] - 1 + 127 - 7, 1), 1, 254)
    codes = (v * np.exp2(127.0 - byte)[:, None, :]).reshape(n, m).astype(np.float32).astype(ml_dtypes.float8_e4m3fn).view(np.uint8)
    words = codes.reshape(n // 512, 128, 4, m).transpose(0, 1, 3, 2)
    return np.ascontiguousarray(words), np.ascontiguousarray(byte.astype(np.uint8).reshape(n // 512, 16, m))


K, T, S, N, H, U = 512, 2048, 512, 512, 512, 1024


def setup_inputs():
    n = np.random.standard_normal
    s = mx_kscale(K)[:, None]
    u = mx_kscale(H)
    packed_xT = pack_weight(n((K, T)) * s)
    packed_w1 = pack_weight(n((K, H)) / np.sqrt(K) / s)
    packed_w2 = pack_weight(n((H, N)) / np.sqrt(H) / u[:, None])
    return {
        "x_words": packed_xT[0],
        "x_scales": packed_xT[1],
        "w1_words": packed_w1[0],
        "w1_scales": packed_w1[1],
        "mem": n((H, U)).astype(np.float32),
        "gn": (np.random.uniform(0.5, 1.5, (H, 1)) * u[:, None]).astype(np.float32),
        "w2_words": packed_w2[0],
        "w2_scales": packed_w2[1],
        "offs": striped8(np.random.randint(0, T, (8, S))),
        "slot": striped8(np.stack([np.random.permutation(U)[:S] for _ in range(8)])),
    }


def reference(x_words, x_scales, w1_words, w1_scales, mem, gn, w2_words, w2_scales, offs, slot):
    xq = unpack_weight(x_words, x_scales)[np.arange(K)[:, None], runs(offs, K)]
    y = unpack_weight(w1_words, w1_scales).T @ xq
    nw = f64(mem)[np.arange(H)[:, None], runs(slot, H)] + 0.75 * (np.tanh(y - (f64(mem)[np.arange(H)[:, None], runs(slot, H)])))
    pg = f64(mem).copy()
    pg[np.arange(H)[:, None], runs(slot, H)] = nw
    z = f64(gn) * pg
    out_0 = unpack_weight(w2_words, w2_scales).T @ mxq(z, 0, "e4m3")
    return (out_0,) + planes(out_0)

@@ -1,0 +1,179 @@
+from contextlib import ExitStack
+
+import concourse.mybir as mybir
+
+K, T, S, N, H, U = 512, 2048, 512, 512, 512, 1024
+FLOPS = 2 * K * H * S + 2 * H * N * U
+
+F32 = mybir.dt.float32
+BF16 = mybir.dt.bfloat16
+I32 = mybir.dt.int32
+U32 = mybir.dt.uint32
+U16 = mybir.dt.uint16
+U8 = mybir.dt.uint8
+FP8X4 = mybir.dt.float8_e4m3fn_x4
+ALU = mybir.AluOpType
+ACT = mybir.ActivationFunctionType
+
+P = 128
+PACK = 4
+CH = 256
+NCH = U // CH
+
+
+def tile_picked_hashpage_none_po_kernel(
+    tc, x_words, x_scales, w1_words, w1_scales, mem, gn, w2_words, w2_scales, offs, slot, out_0, out_1, out_2
+):
+    nc = tc.nc
+
+    def words_of(ap):
+        return ap[0].rearrange("p n t -> p (n t)").bitcast(I32)
+
+    with ExitStack() as ctx:
+        lists = ctx.enter_context(tc.tile_pool(name="lists", bufs=1))
+        keep = ctx.enter_context(tc.tile_pool(name="keep", bufs=1))
+        psum = ctx.enter_context(tc.psum_pool(name="psum", bufs=8))
+
+        offs_sb = lists.tile([P, S // 16], U16, name="offs_sb")
+        slot_sb = lists.tile([P, S // 16], U16, name="slot_sb")
+        nc.sync.dma_start(offs_sb[:], offs)
+        nc.sync.dma_start(slot_sb[:], slot)
+
+        def load_scale_rows(name, src):
+            raw = keep.tile([P, src.shape[2]], U8, name=name, tag="raw_scales", align_bytes=64)
+            nc.gpsimd.memset(raw[:].bitcast(I32), 0)
+            for j in range(4):
+                nc.sync.dma_start(raw[j:P:32, :].bitcast(I32), src[0, j:16:4, :].bitcast(I32))
+            return raw
+
+        def deal(name, raw, dtype):
+            dealt = keep.tile([P, H], dtype, name=name, align_bytes=64)
+            nc.vector.tensor_copy(
+                dealt[:].rearrange("p (t m) -> p m t", t=PACK), raw[:].rearrange("p (m t) -> p m t", t=PACK)
+            )
+            return dealt
+
+        x_scale_table = keep.tile([P, T], U8, name="x_scale_table", tag="reuse_a", align_bytes=64)
+        nc.vector.memset(x_scale_table[:].bitcast(I32), 0)
+        nc.scalar.dma_start(x_scale_table[0:P:8, :].bitcast(I32), x_scales[0].bitcast(I32))
+        w1_scale_raw = load_scale_rows("w1_scale_raw", w1_scales)
+
+        x_word_table = keep.tile([P, T], I32, name="x_word_table", tag="reuse_c", align_bytes=64)
+        nc.sync.dma_start(x_word_table[:], words_of(x_words))
+        w1_word_raw = keep.tile([P, H], I32, name="w1_word_raw", align_bytes=64)
+        nc.sync.dma_start(w1_word_raw[:], words_of(w1_words))
+
+        mem_rows = mem.rearrange("(p t) w -> p t w", t=PACK)
+        page = []
+
+        def load_page(t, tag):
+            pg = keep.tile([P, U], F32, name="page%d" % t, tag=tag, align_bytes=64)
+            nc.sync.dma_start(pg[:], mem_rows[:, t, :])
+            page.append(pg)
+
+        load_page(0, "page0")
+        load_page(1, "page1")
+
+        picked_bytes = keep.tile([P, S], U8, name="picked_bytes", align_bytes=64)
+        nc.vector.tensor_copy(picked_bytes[:], x_scale_table[:].indirect(offs_sb[:]))
+        x_scale = keep.tile([P, S], U8, name="x_scale", align_bytes=64)
+        nc.vector.memset(x_scale[:].bitcast(I32), 0)
+        for j in range(4):
+            nc.scalar.dma_start(x_scale[j:P:32, :].bitcast(I32), picked_bytes[8 * j : P : 32, :].bitcast(I32))
+
+        picked_words = keep.tile([P, S], U32, name="picked_words", align_bytes=64)
+        nc.vector.tensor_copy(picked_words[:], x_word_table[:].bitcast(U32).indirect(offs_sb[:]))
+
+        w1_codes = deal("w1_codes", w1_word_raw, I32)
+        w1_scale = deal("w1_scale", w1_scale_raw, U8)
+
+        load_page(2, "reuse_a")
+        load_page(3, "reuse_c")
+        gain = keep.tile([P, PACK], F32, name="gain")
+        nc.gpsimd.dma_start(gain[:], gn.rearrange("(p t) o -> p (t o)", t=PACK))
+        w2_word_raw = keep.tile([P, N], I32, name="w2_word_raw", tag="w1_word_raw", align_bytes=64)
+        nc.sync.dma_start(w2_word_raw[:], words_of(w2_words))
+        w2_scale_raw = load_scale_rows("w2_scale_raw", w2_scales)
+
+        z_bf = [keep.tile([P, CH, PACK], BF16, name="z_bf%d" % c, align_bytes=64) for c in range(NCH)]
+
+        def scale_rows(t, c):
+            nc.scalar.activation(
+                z_bf[c][:, :, t], page[t][:, c * CH : (c + 1) * CH], ACT.Copy, scale=gain[:, t : t + 1]
+            )
+
+        olds, steps = [], []
+        for t in range(PACK):
+            cols = slice(t * P, (t + 1) * P)
+            y = psum.tile([P, S], F32, name="y%d" % t, tag="bank")
+            nc.tensor.matmul_mx(
+                y[:],
+                lhsT=w1_codes[:, cols].bitcast(FP8X4),
+                lhsT_scale=w1_scale[:, cols],
+                rhs=picked_words[:].bitcast(FP8X4),
+                rhs_scale=x_scale[:],
+                start=True,
+                stop=True,
+            )
+            old = keep.tile([P, S], F32, name="old%d" % t)
+            nc.vector.tensor_copy(old[:], page[t][:].indirect(slot_sb[:]))
+            diff = keep.tile([P, S], F32, name="diff%d" % t)
+            nc.vector.tensor_tensor(diff[:], y[:], old[:], ALU.subtract)
+            pull = keep.tile([P, S], F32, name="pull%d" % t)
+            nc.scalar.activation(pull[:], diff[:], ACT.Tanh)
+            step = keep.tile([P, S], F32, name="step%d" % t)
+            nc.scalar.activation(step[:], pull[:], ACT.Copy, scale=0.75)
+            olds.append(old)
+            steps.append(step)
+
+        w2_codes = deal("w2_codes", w2_word_raw, I32)
+        w2_scale = deal("w2_scale", w2_scale_raw, U8)
+        for t in range(PACK):
+            nc.vector.tensor_tensor(page[t][:].indirect(slot_sb[:]), olds[t][:], steps[t][:], ALU.add)
+            if t < PACK - 1:
+                for c in range(NCH):
+                    scale_rows(t, c)
+
+        out_rows = out_0.rearrange("(p t) w -> p t w", t=PACK)
+        out_words = words_of(out_1)
+        out_scale = keep.tile([P, U], U8, name="out_scale", align_bytes=64)
+        for c in range(NCH):
+            span = slice(c * CH, (c + 1) * CH)
+            scale_rows(PACK - 1, c)
+            z_codes = keep.tile([P, CH], U32, name="z_codes%d" % c, align_bytes=64)
+            z_scale = keep.tile([P, CH], U8, name="z_scale%d" % c, align_bytes=64)
+            nc.vector.quantize_mx(
+                out=z_codes[:].bitcast(FP8X4), scales=z_scale[:], in_=z_bf[c][:].rearrange("p w t -> p (w t)")
+            )
+            res = keep.tile([P, PACK, CH], F32, name="res%d" % c)
+            for half in range(2):
+                acc = psum.tile([P, 2, CH], F32, name="acc%d_%d" % (c, half), tag="bank")
+                for e in range(2):
+                    cols = slice((2 * half + e) * P, (2 * half + e + 1) * P)
+                    nc.tensor.matmul_mx(
+                        acc[:, e, :],
+                        lhsT=w2_codes[:, cols].bitcast(FP8X4),
+                        lhsT_scale=w2_scale[:, cols],
+                        rhs=z_codes[:].bitcast(FP8X4),
+                        rhs_scale=z_scale[:],
+                        start=True,
+                        stop=True,
+                    )
+                if c == 0:
+                    nc.vector.tensor_copy(res[:, 2 * half : 2 * half + 2, :], acc[:])
+                else:
+                    nc.scalar.copy(res[:, 2 * half : 2 * half + 2, :], acc[:])
+            nc.sync.dma_start(out_rows[:, :, span], res[:])
+            res_bf = keep.tile([P, CH, PACK], BF16, name="res_bf%d" % c, align_bytes=64)
+            nc.vector.tensor_copy(
+                res_bf[:].rearrange("p (c i) t -> p c t i", i=4), res[:].rearrange("p t (c i) -> p c t i", i=4)
+            )
+            res_codes = keep.tile([P, CH], I32, name="res_codes%d" % c, align_bytes=64)
+            nc.vector.quantize_mx(
+                out=res_codes[:].bitcast(FP8X4), scales=out_scale[:, span], in_=res_bf[:].rearrange("p w t -> p (w t)")
+            )
+            nc.sync.dma_start(out_words[:, span], res_codes[:])
+        for q in range(4):
+            nc.scalar.dma_start(
+                out_2[0, 4 * q : 4 * q + 4, :].bitcast(I32), out_scale[32 * q : 32 * q + 4, :].bitcast(I32)
+            )

@@ -1,6 +1,7 @@
 from contextlib import ExitStack
 
 import concourse.mybir as mybir
+from concourse.masks import make_identity
 
 K, T, S, N, H, U = 512, 2048, 512, 512, 512, 1024
 FLOPS = 2 * K * H * S + 2 * H * N * U
@@ -17,8 +18,10 @@ ACT = mybir.ActivationFunctionType
 
 P = 128
 PACK = 4
-CH = 256
-NCH = U // CH
+WIDTHS = (128, 256, 256, 256, 128)
+STARTS = tuple(sum(WIDTHS[:c]) for c in range(len(WIDTHS)))
+NCH = len(WIDTHS)
+BANK = 512
 
 
 def tile_picked_hashpage_none_po_kernel(
@@ -36,32 +39,19 @@ def tile_picked_hashpage_none_po_kernel(
 
         offs_sb = lists.tile([P, S // 16], U16, name="offs_sb")
         slot_sb = lists.tile([P, S // 16], U16, name="slot_sb")
-        nc.sync.dma_start(offs_sb[:], offs)
-        nc.sync.dma_start(slot_sb[:], slot)
-
-        def load_scale_rows(name, src):
+        def load_scale_rows(name, src, queue):
             raw = keep.tile([P, src.shape[2]], U8, name=name, tag="raw_scales", align_bytes=64)
             nc.gpsimd.memset(raw[:].bitcast(I32), 0)
             for j in range(4):
-                nc.sync.dma_start(raw[j:P:32, :].bitcast(I32), src[0, j:16:4, :].bitcast(I32))
+                queue.dma_start(raw[j:P:32, :].bitcast(I32), src[0, j:16:4, :].bitcast(I32))
             return raw
 
-        def deal(name, raw, dtype):
-            dealt = keep.tile([P, H], dtype, name=name, align_bytes=64)
+        def deal(name, raw, dtype, tag):
+            dealt = keep.tile([P, H], dtype, name=name, tag=tag, align_bytes=64)
             nc.vector.tensor_copy(
                 dealt[:].rearrange("p (t m) -> p m t", t=PACK), raw[:].rearrange("p (m t) -> p m t", t=PACK)
             )
             return dealt
-
-        x_scale_table = keep.tile([P, T], U8, name="x_scale_table", tag="reuse_a", align_bytes=64)
-        nc.vector.memset(x_scale_table[:].bitcast(I32), 0)
-        nc.scalar.dma_start(x_scale_table[0:P:8, :].bitcast(I32), x_scales[0].bitcast(I32))
-        w1_scale_raw = load_scale_rows("w1_scale_raw", w1_scales)
-
-        x_word_table = keep.tile([P, T], I32, name="x_word_table", tag="reuse_c", align_bytes=64)
-        nc.sync.dma_start(x_word_table[:], words_of(x_words))
-        w1_word_raw = keep.tile([P, H], I32, name="w1_word_raw", align_bytes=64)
-        nc.sync.dma_start(w1_word_raw[:], words_of(w1_words))
 
         mem_rows = mem.rearrange("(p t) w -> p t w", t=PACK)
         page = []
@@ -71,7 +61,17 @@ def tile_picked_hashpage_none_po_kernel(
             nc.sync.dma_start(pg[:], mem_rows[:, t, :])
             page.append(pg)
 
+        nc.sync.dma_start(slot_sb[:], slot)
         load_page(0, "page0")
+        x_scale_table = keep.tile([P, T], U8, name="x_scale_table", tag="reuse_a", align_bytes=64)
+        nc.vector.memset(x_scale_table[:].bitcast(I32), 0)
+        nc.sync.dma_start(x_scale_table[0:P:8, :].bitcast(I32), x_scales[0].bitcast(I32))
+        nc.sync.dma_start(offs_sb[:], offs)
+        x_word_table = keep.tile([P, T], I32, name="x_word_table", tag="reuse_c", align_bytes=64)
+        nc.sync.dma_start(x_word_table[:], words_of(x_words))
+        w1_word_raw = keep.tile([P, H], I32, name="w1_word_raw", align_bytes=64)
+        nc.sync.dma_start(w1_word_raw[:], words_of(w1_words))
+        w1_scale_raw = load_scale_rows("w1_scale_raw", w1_scales, nc.sync)
         load_page(1, "page1")
 
         picked_bytes = keep.tile([P, S], U8, name="picked_bytes", align_bytes=64)
@@ -84,25 +84,28 @@ def tile_picked_hashpage_none_po_kernel(
         picked_words = keep.tile([P, S], U32, name="picked_words", align_bytes=64)
         nc.vector.tensor_copy(picked_words[:], x_word_table[:].bitcast(U32).indirect(offs_sb[:]))
 
-        w1_codes = deal("w1_codes", w1_word_raw, I32)
-        w1_scale = deal("w1_scale", w1_scale_raw, U8)
+        w1_codes = deal("w1_codes", w1_word_raw, I32, "w1_codes")
+        w1_scale = deal("w1_scale", w1_scale_raw, U8, "w1_scale")
 
         load_page(2, "reuse_a")
         load_page(3, "reuse_c")
-        gain = keep.tile([P, PACK], F32, name="gain")
-        nc.gpsimd.dma_start(gain[:], gn.rearrange("(p t) o -> p (t o)", t=PACK))
+        identity = keep.tile([P, P], F32, name="identity")
+        make_identity(nc, identity[:])
         w2_word_raw = keep.tile([P, N], I32, name="w2_word_raw", tag="w1_word_raw", align_bytes=64)
         nc.sync.dma_start(w2_word_raw[:], words_of(w2_words))
-        w2_scale_raw = load_scale_rows("w2_scale_raw", w2_scales)
+        w2_scale_raw = load_scale_rows("w2_scale_raw", w2_scales, nc.sync)
 
-        z_bf = [keep.tile([P, CH, PACK], BF16, name="z_bf%d" % c, align_bytes=64) for c in range(NCH)]
+        z_pairs = [keep.tile([P, 2, WIDTHS[c], 2], BF16, name="z_pairs%d" % c, align_bytes=64) for c in range(NCH)]
 
         def scale_rows(t, c):
             nc.scalar.activation(
-                z_bf[c][:, :, t], page[t][:, c * CH : (c + 1) * CH], ACT.Copy, scale=gain[:, t : t + 1]
+                z_pairs[c][:, t // 2, :, t % 2],
+                page[t][:, STARTS[c] : STARTS[c] + WIDTHS[c]],
+                ACT.Copy,
+                scale=gain[:, t : t + 1],
             )
 
-        olds, steps = [], []
+        ys = []
         for t in range(PACK):
             cols = slice(t * P, (t + 1) * P)
             y = psum.tile([P, S], F32, name="y%d" % t, tag="bank")
@@ -115,41 +118,70 @@ def tile_picked_hashpage_none_po_kernel(
                 start=True,
                 stop=True,
             )
-            old = keep.tile([P, S], F32, name="old%d" % t)
+            ys.append(y)
+
+        olds, steps = [], []
+        for t in range(PACK):
+            old = keep.tile([P, S], F32, name="old%d" % t, align_bytes=64)
             nc.vector.tensor_copy(old[:], page[t][:].indirect(slot_sb[:]))
-            diff = keep.tile([P, S], F32, name="diff%d" % t)
-            nc.vector.tensor_tensor(diff[:], y[:], old[:], ALU.subtract)
             pull = keep.tile([P, S], F32, name="pull%d" % t)
-            nc.scalar.activation(pull[:], diff[:], ACT.Tanh)
-            step = keep.tile([P, S], F32, name="step%d" % t)
-            nc.scalar.activation(step[:], pull[:], ACT.Copy, scale=0.75)
+            step = keep.tile([P, S], F32, name="step%d" % t, align_bytes=64)
+            if t == 0:
+                diff = keep.tile([P, S], F32, name="diff")
+                nc.vector.tensor_tensor(diff[:], ys[t][:], old[:], ALU.subtract)
+                nc.scalar.activation(pull[:], diff[:], ACT.Tanh)
+                nc.scalar.activation(step[:], pull[:], ACT.Copy, scale=0.75)
+            else:
+                minus_y = keep.tile([P, S], F32, name="minus_y%d" % t)
+                nc.scalar.activation(minus_y[:], ys[t][:], ACT.Copy, scale=-1.0)
+                turned = psum.tile([P, S], F32, name="turned%d" % t, tag="bank")
+                for b in range(S // P):
+                    cols = slice(b * P, (b + 1) * P)
+                    nc.tensor.matmul(turned[:, cols], old[:, cols], identity[:], start=True, stop=False, is_transpose=True)
+                    nc.tensor.matmul(turned[:, cols], minus_y[:, cols], identity[:], start=False, stop=True, is_transpose=True)
+                nc.scalar.activation(pull[:], turned[:], ACT.Tanh, scale=-1.0)
+                back = psum.tile([P, S], F32, name="back%d" % t, tag="bank")
+                for b in range(S // P):
+                    cols = slice(b * P, (b + 1) * P)
+                    nc.tensor.transpose(back[:, cols], pull[:, cols], identity[:])
+                nc.scalar.activation(step[:], back[:], ACT.Copy, scale=0.75)
             olds.append(old)
             steps.append(step)
 
-        w2_codes = deal("w2_codes", w2_word_raw, I32)
-        w2_scale = deal("w2_scale", w2_scale_raw, U8)
+        gain = keep.tile([P, PACK], F32, name="gain", tag="minus_y3")
+        nc.sync.dma_start(gain[:], gn.rearrange("(p t) o -> p (t o)", t=PACK))
         for t in range(PACK):
             nc.vector.tensor_tensor(page[t][:].indirect(slot_sb[:]), olds[t][:], steps[t][:], ALU.add)
             if t < PACK - 1:
                 for c in range(NCH):
                     scale_rows(t, c)
 
+        w2_codes = deal("w2_codes", w2_word_raw, I32, "old3")
+        w2_scale = deal("w2_scale", w2_scale_raw, U8, "step3")
         out_rows = out_0.rearrange("(p t) w -> p t w", t=PACK)
         out_words = words_of(out_1)
         out_scale = keep.tile([P, U], U8, name="out_scale", align_bytes=64)
+        res_codes = keep.tile([P, U], I32, name="res_codes", align_bytes=64)
+        accs = []
         for c in range(NCH):
-            span = slice(c * CH, (c + 1) * CH)
+            width = WIDTHS[c]
+            per_bank = BANK // width
             scale_rows(PACK - 1, c)
-            z_codes = keep.tile([P, CH], U32, name="z_codes%d" % c, align_bytes=64)
-            z_scale = keep.tile([P, CH], U8, name="z_scale%d" % c, align_bytes=64)
-            nc.vector.quantize_mx(
-                out=z_codes[:].bitcast(FP8X4), scales=z_scale[:], in_=z_bf[c][:].rearrange("p w t -> p (w t)")
+            z_bf = keep.tile([P, width, PACK], BF16, name="z_bf%d" % c, align_bytes=64)
+            nc.vector.tensor_copy(
+                z_bf[:].rearrange("p w t -> p (w t)").bitcast(F32).rearrange("p (w u) -> p w u", u=2),
+                z_pairs[c][:].rearrange("p u w e -> p (u w e)").bitcast(F32).rearrange("p (u w) -> p w u", u=2),
             )
-            res = keep.tile([P, PACK, CH], F32, name="res%d" % c)
-            for half in range(2):
-                acc = psum.tile([P, 2, CH], F32, name="acc%d_%d" % (c, half), tag="bank")
-                for e in range(2):
-                    cols = slice((2 * half + e) * P, (2 * half + e + 1) * P)
+            z_codes = keep.tile([P, width], U32, name="z_codes%d" % c, align_bytes=64)
+            z_scale = keep.tile([P, width], U8, name="z_scale%d" % c, align_bytes=64)
+            nc.vector.quantize_mx(
+                out=z_codes[:].bitcast(FP8X4), scales=z_scale[:], in_=z_bf[:].rearrange("p w t -> p (w t)")
+            )
+            banks = []
+            for t0 in range(0, PACK, per_bank):
+                acc = psum.tile([P, per_bank, width], F32, name="acc%d_%d" % (c, t0), tag="bank")
+                for e in range(per_bank):
+                    cols = slice((t0 + e) * P, (t0 + e + 1) * P)
                     nc.tensor.matmul_mx(
                         acc[:, e, :],
                         lhsT=w2_codes[:, cols].bitcast(FP8X4),
@@ -159,20 +191,27 @@ def tile_picked_hashpage_none_po_kernel(
                         start=True,
                         stop=True,
                     )
-                if c == 0:
-                    nc.vector.tensor_copy(res[:, 2 * half : 2 * half + 2, :], acc[:])
-                else:
-                    nc.scalar.copy(res[:, 2 * half : 2 * half + 2, :], acc[:])
+                banks.append(acc)
+            accs.append(banks)
+        for c in range(NCH):
+            width = WIDTHS[c]
+            per_bank = BANK // width
+            span = slice(STARTS[c], STARTS[c] + width)
+            res_bf = keep.tile([P, width, PACK], BF16, name="res_bf%d" % c, align_bytes=64)
+            res = keep.tile([P, PACK, width], F32, name="res%d" % c)
+            for b, acc in enumerate(accs[c]):
+                rows = slice(b * per_bank, (b + 1) * per_bank)
+                nc.scalar.copy(res[:, rows, :], acc[:])
             nc.sync.dma_start(out_rows[:, :, span], res[:])
-            res_bf = keep.tile([P, CH, PACK], BF16, name="res_bf%d" % c, align_bytes=64)
             nc.vector.tensor_copy(
                 res_bf[:].rearrange("p (c i) t -> p c t i", i=4), res[:].rearrange("p t (c i) -> p c t i", i=4)
             )
-            res_codes = keep.tile([P, CH], I32, name="res_codes%d" % c, align_bytes=64)
             nc.vector.quantize_mx(
-                out=res_codes[:].bitcast(FP8X4), scales=out_scale[:, span], in_=res_bf[:].rearrange("p w t -> p (w t)")
+                out=res_codes[:, span].bitcast(FP8X4), scales=out_scale[:, span], in_=res_bf[:].rearrange("p w t -> p (w t)")
             )
-            nc.sync.dma_start(out_words[:, span], res_codes[:])
+            if c > 0:
+                done = slice(0 if c == 1 else span.start, span.stop)
+                nc.sync.dma_start(out_words[:, done], res_codes[:, done])
         for q in range(4):
             nc.scalar.dma_start(
                 out_2[0, 4 * q : 4 * q + 4, :].bitcast(I32), out_scale[32 * q : 32 * q + 4, :].bitcast(I32)

@@ -39,8 +39,8 @@ def tile_picked_hashpage_none_po_kernel(
 
         offs_sb = lists.tile([P, S // 16], U16, name="offs_sb")
         slot_sb = lists.tile([P, S // 16], U16, name="slot_sb")
-        def load_scale_rows(name, src, queue):
-            raw = keep.tile([P, src.shape[2]], U8, name=name, tag="raw_scales", align_bytes=64)
+        def load_scale_rows(name, src, queue, tag):
+            raw = keep.tile([P, src.shape[2]], U8, name=name, tag=tag, align_bytes=64)
             nc.gpsimd.memset(raw[:].bitcast(I32), 0)
             for j in range(4):
                 queue.dma_start(raw[j:P:32, :].bitcast(I32), src[0, j:16:4, :].bitcast(I32))
@@ -67,33 +67,33 @@ def tile_picked_hashpage_none_po_kernel(
         nc.vector.memset(x_scale_table[:].bitcast(I32), 0)
         nc.sync.dma_start(x_scale_table[0:P:8, :].bitcast(I32), x_scales[0].bitcast(I32))
         nc.sync.dma_start(offs_sb[:], offs)
-        x_word_table = keep.tile([P, T], I32, name="x_word_table", tag="reuse_c", align_bytes=64)
-        nc.sync.dma_start(x_word_table[:], words_of(x_words))
         w1_word_raw = keep.tile([P, H], I32, name="w1_word_raw", align_bytes=64)
         nc.sync.dma_start(w1_word_raw[:], words_of(w1_words))
-        w1_scale_raw = load_scale_rows("w1_scale_raw", w1_scales, nc.sync)
+        w1_scale_raw = load_scale_rows("w1_scale_raw", w1_scales, nc.gpsimd, "w1_scale_raw")
         load_page(1, "page1")
+        x_word_table = keep.tile([P, T], I32, name="x_word_table", tag="reuse_c", align_bytes=64)
+        nc.sync.dma_start(x_word_table[:], words_of(x_words))
+        load_page(2, "page2")
 
         picked_bytes = keep.tile([P, S], U8, name="picked_bytes", align_bytes=64)
         nc.vector.tensor_copy(picked_bytes[:], x_scale_table[:].indirect(offs_sb[:]))
         x_scale = keep.tile([P, S], U8, name="x_scale", align_bytes=64)
         nc.vector.memset(x_scale[:].bitcast(I32), 0)
         for j in range(4):
-            nc.scalar.dma_start(x_scale[j:P:32, :].bitcast(I32), picked_bytes[8 * j : P : 32, :].bitcast(I32))
+            (nc.scalar, nc.sync)[j % 2].dma_start(x_scale[j:P:32, :].bitcast(I32), picked_bytes[8 * j : P : 32, :].bitcast(I32))
 
         picked_words = keep.tile([P, S], U32, name="picked_words", align_bytes=64)
         nc.vector.tensor_copy(picked_words[:], x_word_table[:].bitcast(U32).indirect(offs_sb[:]))
 
         w1_codes = deal("w1_codes", w1_word_raw, I32, "w1_codes")
-        w1_scale = deal("w1_scale", w1_scale_raw, U8, "w1_scale")
+        w1_scale = deal("w1_scale", w1_scale_raw, U8, "reuse_c")
 
-        load_page(2, "reuse_a")
-        load_page(3, "reuse_c")
+        load_page(3, "reuse_a")
         identity = keep.tile([P, P], F32, name="identity")
         make_identity(nc, identity[:])
         w2_word_raw = keep.tile([P, N], I32, name="w2_word_raw", tag="w1_word_raw", align_bytes=64)
         nc.sync.dma_start(w2_word_raw[:], words_of(w2_words))
-        w2_scale_raw = load_scale_rows("w2_scale_raw", w2_scales, nc.sync)
+        w2_scale_raw = load_scale_rows("w2_scale_raw", w2_scales, nc.sync, "picked_bytes")
 
         z_pairs = [keep.tile([P, 2, WIDTHS[c], 2], BF16, name="z_pairs%d" % c, align_bytes=64) for c in range(NCH)]
 
@@ -105,8 +105,8 @@ def tile_picked_hashpage_none_po_kernel(
                 scale=gain[:, t : t + 1],
             )
 
-        ys = []
-        for t in range(PACK):
+        ys = {}
+        for t in (1, 0, 2, 3):
             cols = slice(t * P, (t + 1) * P)
             y = psum.tile([P, S], F32, name="y%d" % t, tag="bank")
             nc.tensor.matmul_mx(
@@ -118,21 +118,25 @@ def tile_picked_hashpage_none_po_kernel(
                 start=True,
                 stop=True,
             )
-            ys.append(y)
+            ys[t] = y
 
         olds, steps = [], []
         for t in range(PACK):
-            old = keep.tile([P, S], F32, name="old%d" % t, align_bytes=64)
+            old = keep.tile([P, S], F32, name="old%d" % t, tag="w1_scale_raw" if t == 2 else "old%d" % t, align_bytes=64)
             nc.vector.tensor_copy(old[:], page[t][:].indirect(slot_sb[:]))
-            pull = keep.tile([P, S], F32, name="pull%d" % t)
+            pull = keep.tile([P, S], F32, name="pull%d" % t, tag="diff" if t == 1 else "pull%d" % t)
             step = keep.tile([P, S], F32, name="step%d" % t, align_bytes=64)
             if t == 0:
                 diff = keep.tile([P, S], F32, name="diff")
-                nc.vector.tensor_tensor(diff[:], ys[t][:], old[:], ALU.subtract)
-                nc.scalar.activation(pull[:], diff[:], ACT.Tanh)
-                nc.scalar.activation(step[:], pull[:], ACT.Copy, scale=0.75)
+                halves = (slice(0, S // 2), slice(S // 2, S))
+                for half in halves:
+                    nc.vector.tensor_tensor(diff[:, half], ys[t][:, half], old[:, half], ALU.subtract)
+                for half in halves:
+                    nc.scalar.activation(pull[:, half], diff[:, half], ACT.Tanh)
+                for half in halves:
+                    nc.scalar.activation(step[:, half], pull[:, half], ACT.Copy, scale=0.75)
             else:
-                minus_y = keep.tile([P, S], F32, name="minus_y%d" % t)
+                minus_y = keep.tile([P, S], F32, name="minus_y%d" % t, tag={1: "minus_y1", 2: "pull0", 3: "minus_y1"}[t])
                 nc.scalar.activation(minus_y[:], ys[t][:], ACT.Copy, scale=-1.0)
                 turned = psum.tile([P, S], F32, name="turned%d" % t, tag="bank")
                 for b in range(S // P):
@@ -148,7 +152,7 @@ def tile_picked_hashpage_none_po_kernel(
             olds.append(old)
             steps.append(step)
 
-        gain = keep.tile([P, PACK], F32, name="gain", tag="minus_y3")
+        gain = keep.tile([P, PACK], F32, name="gain", tag="minus_y1")
         nc.sync.dma_start(gain[:], gn.rearrange("(p t) o -> p (t o)", t=PACK))
         for t in range(PACK):
             nc.vector.tensor_tensor(page[t][:].indirect(slot_sb[:]), olds[t][:], steps[t][:], ALU.add)
@@ -201,7 +205,10 @@ def tile_picked_hashpage_none_po_kernel(
             res = keep.tile([P, PACK, width], F32, name="res%d" % c)
             for b, acc in enumerate(accs[c]):
                 rows = slice(b * per_bank, (b + 1) * per_bank)
-                nc.scalar.copy(res[:, rows, :], acc[:])
+                if (c, b) == (2, 0):
+                    nc.vector.tensor_copy(res[:, rows, :], acc[:])
+                else:
+                    nc.scalar.copy(res[:, rows, :], acc[:])
             nc.sync.dma_start(out_rows[:, :, span], res[:])
             nc.vector.tensor_copy(
                 res_bf[:].rearrange("p (c i) t -> p c t i", i=4), res[:].rearrange("p t (c i) -> p c t i", i=4)

@@ -18,10 +18,18 @@ ACT = mybir.ActivationFunctionType
 
 P = 128
 PACK = 4
+QUADRANT = 32
+BLOCK_PARTITIONS = 8
+LIST_PARTITIONS = 16
+BANK = 512
+BANKS = 8
+RATE = 0.75
+
 WIDTHS = (128, 256, 256, 256, 128)
 STARTS = tuple(sum(WIDTHS[:c]) for c in range(len(WIDTHS)))
-NCH = len(WIDTHS)
-BANK = 512
+CHUNKS = len(WIDTHS)
+VECTOR_BANK = (2, 0)
+BANKWISE_CHUNK = 1
 
 
 def tile_picked_hashpage_none_po_kernel(
@@ -29,21 +37,22 @@ def tile_picked_hashpage_none_po_kernel(
 ):
     nc = tc.nc
 
-    def words_of(ap):
-        return ap[0].rearrange("p n t -> p (n t)").bitcast(I32)
+    def words_of(packed):
+        return packed[0].rearrange("p n t -> p (n t)").bitcast(I32)
 
     with ExitStack() as ctx:
         lists = ctx.enter_context(tc.tile_pool(name="lists", bufs=1))
         keep = ctx.enter_context(tc.tile_pool(name="keep", bufs=1))
-        psum = ctx.enter_context(tc.psum_pool(name="psum", bufs=8))
+        psum = ctx.enter_context(tc.psum_pool(name="psum", bufs=BANKS))
 
-        offs_sb = lists.tile([P, S // 16], U16, name="offs_sb")
-        slot_sb = lists.tile([P, S // 16], U16, name="slot_sb")
-        def load_scale_rows(name, src, queue, tag):
-            raw = keep.tile([P, src.shape[2]], U8, name=name, tag=tag, align_bytes=64)
+        offs_sb = lists.tile([P, S // LIST_PARTITIONS], U16, name="offs_sb")
+        slot_sb = lists.tile([P, S // LIST_PARTITIONS], U16, name="slot_sb")
+
+        def load_scale_rows(name, scales, queue, tag):
+            raw = keep.tile([P, scales.shape[2]], U8, name=name, tag=tag, align_bytes=64)
             nc.gpsimd.memset(raw[:].bitcast(I32), 0)
-            for j in range(4):
-                queue.dma_start(raw[j:P:32, :].bitcast(I32), src[0, j:16:4, :].bitcast(I32))
+            for j in range(PACK):
+                queue.dma_start(raw[j:P:QUADRANT, :].bitcast(I32), scales[0, j : K // QUADRANT : PACK, :].bitcast(I32))
             return raw
 
         def deal(name, raw, dtype, tag):
@@ -57,21 +66,21 @@ def tile_picked_hashpage_none_po_kernel(
         page = []
 
         def load_page(t, tag):
-            pg = keep.tile([P, U], F32, name="page%d" % t, tag=tag, align_bytes=64)
-            nc.sync.dma_start(pg[:], mem_rows[:, t, :])
-            page.append(pg)
+            rows = keep.tile([P, U], F32, name="page%d" % t, tag=tag, align_bytes=64)
+            nc.sync.dma_start(rows[:], mem_rows[:, t, :])
+            page.append(rows)
 
         nc.sync.dma_start(slot_sb[:], slot)
         load_page(0, "page0")
-        x_scale_table = keep.tile([P, T], U8, name="x_scale_table", tag="reuse_a", align_bytes=64)
+        x_scale_table = keep.tile([P, T], U8, name="x_scale_table", align_bytes=64)
         nc.vector.memset(x_scale_table[:].bitcast(I32), 0)
-        nc.sync.dma_start(x_scale_table[0:P:8, :].bitcast(I32), x_scales[0].bitcast(I32))
+        nc.sync.dma_start(x_scale_table[0:P:BLOCK_PARTITIONS, :].bitcast(I32), x_scales[0].bitcast(I32))
         nc.sync.dma_start(offs_sb[:], offs)
         w1_word_raw = keep.tile([P, H], I32, name="w1_word_raw", align_bytes=64)
         nc.sync.dma_start(w1_word_raw[:], words_of(w1_words))
         w1_scale_raw = load_scale_rows("w1_scale_raw", w1_scales, nc.gpsimd, "w1_scale_raw")
         load_page(1, "page1")
-        x_word_table = keep.tile([P, T], I32, name="x_word_table", tag="reuse_c", align_bytes=64)
+        x_word_table = keep.tile([P, T], I32, name="x_word_table", align_bytes=64)
         nc.sync.dma_start(x_word_table[:], words_of(x_words))
         load_page(2, "page2")
 
@@ -79,23 +88,26 @@ def tile_picked_hashpage_none_po_kernel(
         nc.vector.tensor_copy(picked_bytes[:], x_scale_table[:].indirect(offs_sb[:]))
         x_scale = keep.tile([P, S], U8, name="x_scale", align_bytes=64)
         nc.vector.memset(x_scale[:].bitcast(I32), 0)
-        for j in range(4):
-            (nc.scalar, nc.sync)[j % 2].dma_start(x_scale[j:P:32, :].bitcast(I32), picked_bytes[8 * j : P : 32, :].bitcast(I32))
+        for j in range(PACK):
+            (nc.scalar, nc.sync)[j % 2].dma_start(
+                x_scale[j:P:QUADRANT, :].bitcast(I32),
+                picked_bytes[BLOCK_PARTITIONS * j : P : QUADRANT, :].bitcast(I32),
+            )
 
         picked_words = keep.tile([P, S], U32, name="picked_words", align_bytes=64)
         nc.vector.tensor_copy(picked_words[:], x_word_table[:].bitcast(U32).indirect(offs_sb[:]))
 
         w1_codes = deal("w1_codes", w1_word_raw, I32, "w1_codes")
-        w1_scale = deal("w1_scale", w1_scale_raw, U8, "reuse_c")
+        w1_scale = deal("w1_scale", w1_scale_raw, U8, "x_word_table")
 
-        load_page(3, "reuse_a")
+        load_page(3, "x_scale_table")
         identity = keep.tile([P, P], F32, name="identity")
         make_identity(nc, identity[:])
         w2_word_raw = keep.tile([P, N], I32, name="w2_word_raw", tag="w1_word_raw", align_bytes=64)
         nc.sync.dma_start(w2_word_raw[:], words_of(w2_words))
         w2_scale_raw = load_scale_rows("w2_scale_raw", w2_scales, nc.sync, "picked_bytes")
 
-        z_pairs = [keep.tile([P, 2, WIDTHS[c], 2], BF16, name="z_pairs%d" % c, align_bytes=64) for c in range(NCH)]
+        z_pairs = [keep.tile([P, 2, WIDTHS[c], 2], BF16, name="z_pairs%d" % c, align_bytes=64) for c in range(CHUNKS)]
 
         def scale_rows(t, c):
             nc.scalar.activation(
@@ -120,66 +132,85 @@ def tile_picked_hashpage_none_po_kernel(
             )
             ys[t] = y
 
-        olds, steps = [], []
-        for t in range(PACK):
-            old = keep.tile([P, S], F32, name="old%d" % t, tag="w1_scale_raw" if t == 2 else "old%d" % t, align_bytes=64)
+        def look_up(t, tag):
+            old = keep.tile([P, S], F32, name="old%d" % t, tag=tag, align_bytes=64)
             nc.vector.tensor_copy(old[:], page[t][:].indirect(slot_sb[:]))
-            pull = keep.tile([P, S], F32, name="pull%d" % t, tag="diff" if t == 1 else "pull%d" % t)
-            step = keep.tile([P, S], F32, name="step%d" % t, align_bytes=64)
-            if t == 0:
-                diff = keep.tile([P, S], F32, name="diff")
-                halves = (slice(0, S // 2), slice(S // 2, S))
-                for half in halves:
-                    nc.vector.tensor_tensor(diff[:, half], ys[t][:, half], old[:, half], ALU.subtract)
-                for half in halves:
-                    nc.scalar.activation(pull[:, half], diff[:, half], ACT.Tanh)
-                for half in halves:
-                    nc.scalar.activation(step[:, half], pull[:, half], ACT.Copy, scale=0.75)
-            else:
-                minus_y = keep.tile([P, S], F32, name="minus_y%d" % t, tag={1: "minus_y1", 2: "pull0", 3: "minus_y1"}[t])
-                nc.scalar.activation(minus_y[:], ys[t][:], ACT.Copy, scale=-1.0)
-                turned = psum.tile([P, S], F32, name="turned%d" % t, tag="bank")
-                for b in range(S // P):
-                    cols = slice(b * P, (b + 1) * P)
-                    nc.tensor.matmul(turned[:, cols], old[:, cols], identity[:], start=True, stop=False, is_transpose=True)
-                    nc.tensor.matmul(turned[:, cols], minus_y[:, cols], identity[:], start=False, stop=True, is_transpose=True)
-                nc.scalar.activation(pull[:], turned[:], ACT.Tanh, scale=-1.0)
-                back = psum.tile([P, S], F32, name="back%d" % t, tag="bank")
-                for b in range(S // P):
-                    cols = slice(b * P, (b + 1) * P)
-                    nc.tensor.transpose(back[:, cols], pull[:, cols], identity[:])
-                nc.scalar.activation(step[:], back[:], ACT.Copy, scale=0.75)
-            olds.append(old)
-            steps.append(step)
+            return old
 
-        gain = keep.tile([P, PACK], F32, name="gain", tag="minus_y1")
+        def step_direct(t, old):
+            pull = keep.tile([P, S], F32, name="pull%d" % t)
+            step = keep.tile([P, S], F32, name="step%d" % t, align_bytes=64)
+            diff = keep.tile([P, S], F32, name="diff")
+            halves = (slice(0, S // 2), slice(S // 2, S))
+            for half in halves:
+                nc.vector.tensor_tensor(diff[:, half], ys[t][:, half], old[:, half], ALU.subtract)
+            for half in halves:
+                nc.scalar.activation(pull[:, half], diff[:, half], ACT.Tanh)
+            for half in halves:
+                nc.scalar.activation(step[:, half], pull[:, half], ACT.Copy, scale=RATE)
+            return step
+
+        def step_turned(t, old, pull_tag, minus_y_tag):
+            pull = keep.tile([P, S], F32, name="pull%d" % t, tag=pull_tag)
+            step = keep.tile([P, S], F32, name="step%d" % t, align_bytes=64)
+            minus_y = keep.tile([P, S], F32, name="minus_y%d" % t, tag=minus_y_tag)
+            nc.scalar.activation(minus_y[:], ys[t][:], ACT.Copy, scale=-1.0)
+            turned = psum.tile([P, S], F32, name="turned%d" % t, tag="bank")
+            for b in range(S // P):
+                cols = slice(b * P, (b + 1) * P)
+                nc.tensor.matmul(turned[:, cols], old[:, cols], identity[:], start=True, stop=False, is_transpose=True)
+                nc.tensor.matmul(
+                    turned[:, cols], minus_y[:, cols], identity[:], start=False, stop=True, is_transpose=True
+                )
+            nc.scalar.activation(pull[:], turned[:], ACT.Tanh, scale=-1.0)
+            back = psum.tile([P, S], F32, name="back%d" % t, tag="bank")
+            for b in range(S // P):
+                cols = slice(b * P, (b + 1) * P)
+                nc.tensor.transpose(back[:, cols], pull[:, cols], identity[:])
+            nc.scalar.activation(step[:], back[:], ACT.Copy, scale=RATE)
+            return step
+
+        olds = [look_up(0, "old0")]
+        steps = [step_direct(0, olds[0])]
+        olds.append(look_up(1, "old1"))
+        steps.append(step_turned(1, olds[1], pull_tag="diff", minus_y_tag="minus_y1"))
+        olds.append(look_up(2, "w1_scale_raw"))
+        steps.append(step_turned(2, olds[2], pull_tag="pull2", minus_y_tag="pull0"))
+        olds.append(look_up(3, "old3"))
+        steps.append(step_turned(3, olds[3], pull_tag="pull3", minus_y_tag="minus_y1"))
+
+        gain = keep.tile([P, PACK], F32, name="gain", tag="pull0")
         nc.sync.dma_start(gain[:], gn.rearrange("(p t) o -> p (t o)", t=PACK))
+
         for t in range(PACK):
             nc.vector.tensor_tensor(page[t][:].indirect(slot_sb[:]), olds[t][:], steps[t][:], ALU.add)
             if t < PACK - 1:
-                for c in range(NCH):
+                for c in range(CHUNKS):
                     scale_rows(t, c)
 
         w2_codes = deal("w2_codes", w2_word_raw, I32, "old3")
-        w2_scale = deal("w2_scale", w2_scale_raw, U8, "step3")
         out_rows = out_0.rearrange("(p t) w -> p t w", t=PACK)
         out_words = words_of(out_1)
         out_scale = keep.tile([P, U], U8, name="out_scale", align_bytes=64)
-        res_codes = keep.tile([P, U], I32, name="res_codes", align_bytes=64)
-        accs = []
-        for c in range(NCH):
-            width = WIDTHS[c]
-            per_bank = BANK // width
+        out_codes = keep.tile([P, U], I32, name="out_codes", align_bytes=64)
+        z_woven, accs, out_woven = [], [], []
+
+        def weave_z(c):
             scale_rows(PACK - 1, c)
-            z_bf = keep.tile([P, width, PACK], BF16, name="z_bf%d" % c, align_bytes=64)
+            woven = keep.tile([P, WIDTHS[c], PACK], BF16, name="z_woven%d" % c, align_bytes=64)
             nc.vector.tensor_copy(
-                z_bf[:].rearrange("p w t -> p (w t)").bitcast(F32).rearrange("p (w u) -> p w u", u=2),
+                woven[:].rearrange("p w t -> p (w t)").bitcast(F32).rearrange("p (w u) -> p w u", u=2),
                 z_pairs[c][:].rearrange("p u w e -> p (u w e)").bitcast(F32).rearrange("p (u w) -> p w u", u=2),
             )
+            z_woven.append(woven)
+
+        def multiply(c):
+            width = WIDTHS[c]
+            per_bank = BANK // width
             z_codes = keep.tile([P, width], U32, name="z_codes%d" % c, align_bytes=64)
             z_scale = keep.tile([P, width], U8, name="z_scale%d" % c, align_bytes=64)
             nc.vector.quantize_mx(
-                out=z_codes[:].bitcast(FP8X4), scales=z_scale[:], in_=z_bf[:].rearrange("p w t -> p (w t)")
+                out=z_codes[:].bitcast(FP8X4), scales=z_scale[:], in_=z_woven[c][:].rearrange("p w t -> p (w t)")
             )
             banks = []
             for t0 in range(0, PACK, per_bank):
@@ -197,29 +228,52 @@ def tile_picked_hashpage_none_po_kernel(
                     )
                 banks.append(acc)
             accs.append(banks)
-        for c in range(NCH):
+
+        def store_values(c):
             width = WIDTHS[c]
             per_bank = BANK // width
             span = slice(STARTS[c], STARTS[c] + width)
-            res_bf = keep.tile([P, width, PACK], BF16, name="res_bf%d" % c, align_bytes=64)
-            res = keep.tile([P, PACK, width], F32, name="res%d" % c)
+            values = keep.tile([P, PACK, width], F32, name="values%d" % c)
             for b, acc in enumerate(accs[c]):
                 rows = slice(b * per_bank, (b + 1) * per_bank)
-                if (c, b) == (2, 0):
-                    nc.vector.tensor_copy(res[:, rows, :], acc[:])
+                if (c, b) == VECTOR_BANK:
+                    nc.vector.tensor_copy(values[:, rows, :], acc[:])
                 else:
-                    nc.scalar.copy(res[:, rows, :], acc[:])
-            nc.sync.dma_start(out_rows[:, :, span], res[:])
+                    nc.scalar.copy(values[:, rows, :], acc[:])
+                if c == BANKWISE_CHUNK:
+                    nc.sync.dma_start(out_rows[:, rows, span], values[:, rows, :])
+            if c != BANKWISE_CHUNK:
+                nc.sync.dma_start(out_rows[:, :, span], values[:])
+            woven = keep.tile([P, width, PACK], BF16, name="out_woven%d" % c, align_bytes=64)
             nc.vector.tensor_copy(
-                res_bf[:].rearrange("p (c i) t -> p c t i", i=4), res[:].rearrange("p t (c i) -> p c t i", i=4)
+                woven[:].rearrange("p (g i) t -> p g t i", i=4), values[:].rearrange("p t (g i) -> p g t i", i=4)
             )
+            out_woven.append(woven)
+
+        def store_codes(c):
+            span = slice(STARTS[c], STARTS[c] + WIDTHS[c])
             nc.vector.quantize_mx(
-                out=res_codes[:, span].bitcast(FP8X4), scales=out_scale[:, span], in_=res_bf[:].rearrange("p w t -> p (w t)")
+                out=out_codes[:, span].bitcast(FP8X4),
+                scales=out_scale[:, span],
+                in_=out_woven[c][:].rearrange("p w t -> p (w t)"),
             )
             if c > 0:
-                done = slice(0 if c == 1 else span.start, span.stop)
-                nc.sync.dma_start(out_words[:, done], res_codes[:, done])
-        for q in range(4):
+                unstored = slice(0 if c == 1 else span.start, span.stop)
+                nc.sync.dma_start(out_words[:, unstored], out_codes[:, unstored])
+
+        weave_z(0)
+        w2_scale = deal("w2_scale", w2_scale_raw, U8, "step3")
+        multiply(0)
+        weave_z(1)
+        for c in range(2, CHUNKS):
+            weave_z(c)
+            multiply(c - 1)
+        multiply(CHUNKS - 1)
+        for c in range(CHUNKS):
+            store_values(c)
+            store_codes(c)
+        for q in range(P // QUADRANT):
             nc.scalar.dma_start(
-                out_2[0, 4 * q : 4 * q + 4, :].bitcast(I32), out_scale[32 * q : 32 * q + 4, :].bitcast(I32)
+                out_2[0, PACK * q : PACK * (q + 1), :].bitcast(I32),
+                out_scale[QUADRANT * q : QUADRANT * q + PACK, :].bitcast(I32),
             )

from contextlib import ExitStack

import concourse.mybir as mybir
from concourse.masks import make_identity

K, T, S, N, H, U = 512, 2048, 512, 512, 512, 1024
FLOPS = 2 * K * H * S + 2 * H * N * U

F32 = mybir.dt.float32
BF16 = mybir.dt.bfloat16
I32 = mybir.dt.int32
U32 = mybir.dt.uint32
U16 = mybir.dt.uint16
U8 = mybir.dt.uint8
FP8X4 = mybir.dt.float8_e4m3fn_x4
ALU = mybir.AluOpType
ACT = mybir.ActivationFunctionType

P = 128
PACK = 4
QUADRANT = 32
BLOCK_PARTITIONS = 8
LIST_PARTITIONS = 16
BANK = 512
BANKS = 8
RATE = 0.75

WIDTHS = (128, 256, 256, 256, 128)
STARTS = tuple(sum(WIDTHS[:c]) for c in range(len(WIDTHS)))
CHUNKS = len(WIDTHS)
VECTOR_BANK = (2, 0)
BANKWISE_CHUNK = 1


def tile_picked_hashpage_none_po_kernel(
    tc, x_words, x_scales, w1_words, w1_scales, mem, gn, w2_words, w2_scales, offs, slot, out_0, out_1, out_2
):
    nc = tc.nc

    def words_of(packed):
        return packed[0].rearrange("p n t -> p (n t)").bitcast(I32)

    with ExitStack() as ctx:
        lists = ctx.enter_context(tc.tile_pool(name="lists", bufs=1))
        keep = ctx.enter_context(tc.tile_pool(name="keep", bufs=1))
        psum = ctx.enter_context(tc.psum_pool(name="psum", bufs=BANKS))

        offs_sb = lists.tile([P, S // LIST_PARTITIONS], U16, name="offs_sb")
        slot_sb = lists.tile([P, S // LIST_PARTITIONS], U16, name="slot_sb")

        def load_scale_rows(name, scales, queue, tag):
            raw = keep.tile([P, scales.shape[2]], U8, name=name, tag=tag, align_bytes=64)
            nc.gpsimd.memset(raw[:].bitcast(I32), 0)
            for j in range(PACK):
                queue.dma_start(raw[j:P:QUADRANT, :].bitcast(I32), scales[0, j : K // QUADRANT : PACK, :].bitcast(I32))
            return raw

        def deal(name, raw, dtype, tag):
            dealt = keep.tile([P, H], dtype, name=name, tag=tag, align_bytes=64)
            nc.vector.tensor_copy(
                dealt[:].rearrange("p (t m) -> p m t", t=PACK), raw[:].rearrange("p (m t) -> p m t", t=PACK)
            )
            return dealt

        mem_rows = mem.rearrange("(p t) w -> p t w", t=PACK)
        page = []

        def load_page(t, tag):
            rows = keep.tile([P, U], F32, name="page%d" % t, tag=tag, align_bytes=64)
            nc.sync.dma_start(rows[:], mem_rows[:, t, :])
            page.append(rows)

        nc.sync.dma_start(slot_sb[:], slot)
        load_page(0, "page0")
        x_scale_table = keep.tile([P, T], U8, name="x_scale_table", align_bytes=64)
        nc.vector.memset(x_scale_table[:].bitcast(I32), 0)
        nc.sync.dma_start(x_scale_table[0:P:BLOCK_PARTITIONS, :].bitcast(I32), x_scales[0].bitcast(I32))
        nc.sync.dma_start(offs_sb[:], offs)
        w1_word_raw = keep.tile([P, H], I32, name="w1_word_raw", align_bytes=64)
        nc.sync.dma_start(w1_word_raw[:], words_of(w1_words))
        w1_scale_raw = load_scale_rows("w1_scale_raw", w1_scales, nc.gpsimd, "w1_scale_raw")
        load_page(1, "page1")
        x_word_table = keep.tile([P, T], I32, name="x_word_table", align_bytes=64)
        nc.sync.dma_start(x_word_table[:], words_of(x_words))
        load_page(2, "page2")

        picked_bytes = keep.tile([P, S], U8, name="picked_bytes", align_bytes=64)
        nc.vector.tensor_copy(picked_bytes[:], x_scale_table[:].indirect(offs_sb[:]))
        x_scale = keep.tile([P, S], U8, name="x_scale", align_bytes=64)
        nc.vector.memset(x_scale[:].bitcast(I32), 0)
        for j in range(PACK):
            (nc.scalar, nc.sync)[j % 2].dma_start(
                x_scale[j:P:QUADRANT, :].bitcast(I32),
                picked_bytes[BLOCK_PARTITIONS * j : P : QUADRANT, :].bitcast(I32),
            )

        picked_words = keep.tile([P, S], U32, name="picked_words", align_bytes=64)
        nc.vector.tensor_copy(picked_words[:], x_word_table[:].bitcast(U32).indirect(offs_sb[:]))

        w1_codes = deal("w1_codes", w1_word_raw, I32, "w1_codes")
        w1_scale = deal("w1_scale", w1_scale_raw, U8, "x_word_table")

        load_page(3, "x_scale_table")
        identity = keep.tile([P, P], F32, name="identity")
        make_identity(nc, identity[:])
        w2_word_raw = keep.tile([P, N], I32, name="w2_word_raw", tag="w1_word_raw", align_bytes=64)
        nc.sync.dma_start(w2_word_raw[:], words_of(w2_words))
        w2_scale_raw = load_scale_rows("w2_scale_raw", w2_scales, nc.sync, "picked_bytes")

        z_pairs = [keep.tile([P, 2, WIDTHS[c], 2], BF16, name="z_pairs%d" % c, align_bytes=64) for c in range(CHUNKS)]

        def scale_rows(t, c):
            nc.scalar.activation(
                z_pairs[c][:, t // 2, :, t % 2],
                page[t][:, STARTS[c] : STARTS[c] + WIDTHS[c]],
                ACT.Copy,
                scale=gain[:, t : t + 1],
            )

        ys = {}
        for t in (1, 0, 2, 3):
            cols = slice(t * P, (t + 1) * P)
            y = psum.tile([P, S], F32, name="y%d" % t, tag="bank")
            nc.tensor.matmul_mx(
                y[:],
                lhsT=w1_codes[:, cols].bitcast(FP8X4),
                lhsT_scale=w1_scale[:, cols],
                rhs=picked_words[:].bitcast(FP8X4),
                rhs_scale=x_scale[:],
                start=True,
                stop=True,
            )
            ys[t] = y

        def look_up(t, tag):
            old = keep.tile([P, S], F32, name="old%d" % t, tag=tag, align_bytes=64)
            nc.vector.tensor_copy(old[:], page[t][:].indirect(slot_sb[:]))
            return old

        def step_direct(t, old):
            pull = keep.tile([P, S], F32, name="pull%d" % t)
            step = keep.tile([P, S], F32, name="step%d" % t, align_bytes=64)
            diff = keep.tile([P, S], F32, name="diff")
            halves = (slice(0, S // 2), slice(S // 2, S))
            for half in halves:
                nc.vector.tensor_tensor(diff[:, half], ys[t][:, half], old[:, half], ALU.subtract)
            for half in halves:
                nc.scalar.activation(pull[:, half], diff[:, half], ACT.Tanh)
            for half in halves:
                nc.scalar.activation(step[:, half], pull[:, half], ACT.Copy, scale=RATE)
            return step

        def step_turned(t, old, pull_tag, minus_y_tag):
            pull = keep.tile([P, S], F32, name="pull%d" % t, tag=pull_tag)
            step = keep.tile([P, S], F32, name="step%d" % t, align_bytes=64)
            minus_y = keep.tile([P, S], F32, name="minus_y%d" % t, tag=minus_y_tag)
            nc.scalar.activation(minus_y[:], ys[t][:], ACT.Copy, scale=-1.0)
            turned = psum.tile([P, S], F32, name="turned%d" % t, tag="bank")
            for b in range(S // P):
                cols = slice(b * P, (b + 1) * P)
                nc.tensor.matmul(turned[:, cols], old[:, cols], identity[:], start=True, stop=False, is_transpose=True)
                nc.tensor.matmul(
                    turned[:, cols], minus_y[:, cols], identity[:], start=False, stop=True, is_transpose=True
                )
            nc.scalar.activation(pull[:], turned[:], ACT.Tanh, scale=-1.0)
            back = psum.tile([P, S], F32, name="back%d" % t, tag="bank")
            for b in range(S // P):
                cols = slice(b * P, (b + 1) * P)
                nc.tensor.transpose(back[:, cols], pull[:, cols], identity[:])
            nc.scalar.activation(step[:], back[:], ACT.Copy, scale=RATE)
            return step

        olds = [look_up(0, "old0")]
        steps = [step_direct(0, olds[0])]
        olds.append(look_up(1, "old1"))
        steps.append(step_turned(1, olds[1], pull_tag="diff", minus_y_tag="minus_y1"))
        olds.append(look_up(2, "w1_scale_raw"))
        steps.append(step_turned(2, olds[2], pull_tag="pull2", minus_y_tag="pull0"))
        olds.append(look_up(3, "old3"))
        steps.append(step_turned(3, olds[3], pull_tag="pull3", minus_y_tag="minus_y1"))

        gain = keep.tile([P, PACK], F32, name="gain", tag="pull0")
        nc.sync.dma_start(gain[:], gn.rearrange("(p t) o -> p (t o)", t=PACK))

        for t in range(PACK):
            nc.vector.tensor_tensor(page[t][:].indirect(slot_sb[:]), olds[t][:], steps[t][:], ALU.add)
            if t < PACK - 1:
                for c in range(CHUNKS):
                    scale_rows(t, c)

        w2_codes = deal("w2_codes", w2_word_raw, I32, "old3")
        out_rows = out_0.rearrange("(p t) w -> p t w", t=PACK)
        out_words = words_of(out_1)
        out_scale = keep.tile([P, U], U8, name="out_scale", align_bytes=64)
        out_codes = keep.tile([P, U], I32, name="out_codes", align_bytes=64)
        z_woven, accs, out_woven = [], [], []

        def weave_z(c):
            scale_rows(PACK - 1, c)
            woven = keep.tile([P, WIDTHS[c], PACK], BF16, name="z_woven%d" % c, align_bytes=64)
            nc.vector.tensor_copy(
                woven[:].rearrange("p w t -> p (w t)").bitcast(F32).rearrange("p (w u) -> p w u", u=2),
                z_pairs[c][:].rearrange("p u w e -> p (u w e)").bitcast(F32).rearrange("p (u w) -> p w u", u=2),
            )
            z_woven.append(woven)

        def multiply(c):
            width = WIDTHS[c]
            per_bank = BANK // width
            z_codes = keep.tile([P, width], U32, name="z_codes%d" % c, align_bytes=64)
            z_scale = keep.tile([P, width], U8, name="z_scale%d" % c, align_bytes=64)
            nc.vector.quantize_mx(
                out=z_codes[:].bitcast(FP8X4), scales=z_scale[:], in_=z_woven[c][:].rearrange("p w t -> p (w t)")
            )
            banks = []
            for t0 in range(0, PACK, per_bank):
                acc = psum.tile([P, per_bank, width], F32, name="acc%d_%d" % (c, t0), tag="bank")
                for e in range(per_bank):
                    cols = slice((t0 + e) * P, (t0 + e + 1) * P)
                    nc.tensor.matmul_mx(
                        acc[:, e, :],
                        lhsT=w2_codes[:, cols].bitcast(FP8X4),
                        lhsT_scale=w2_scale[:, cols],
                        rhs=z_codes[:].bitcast(FP8X4),
                        rhs_scale=z_scale[:],
                        start=True,
                        stop=True,
                    )
                banks.append(acc)
            accs.append(banks)

        def store_values(c):
            width = WIDTHS[c]
            per_bank = BANK // width
            span = slice(STARTS[c], STARTS[c] + width)
            values = keep.tile([P, PACK, width], F32, name="values%d" % c)
            for b, acc in enumerate(accs[c]):
                rows = slice(b * per_bank, (b + 1) * per_bank)
                if (c, b) == VECTOR_BANK:
                    nc.vector.tensor_copy(values[:, rows, :], acc[:])
                else:
                    nc.scalar.copy(values[:, rows, :], acc[:])
                if c == BANKWISE_CHUNK:
                    nc.sync.dma_start(out_rows[:, rows, span], values[:, rows, :])
            if c != BANKWISE_CHUNK:
                nc.sync.dma_start(out_rows[:, :, span], values[:])
            woven = keep.tile([P, width, PACK], BF16, name="out_woven%d" % c, align_bytes=64)
            nc.vector.tensor_copy(
                woven[:].rearrange("p (g i) t -> p g t i", i=4), values[:].rearrange("p t (g i) -> p g t i", i=4)
            )
            out_woven.append(woven)

        def store_codes(c):
            span = slice(STARTS[c], STARTS[c] + WIDTHS[c])
            nc.vector.quantize_mx(
                out=out_codes[:, span].bitcast(FP8X4),
                scales=out_scale[:, span],
                in_=out_woven[c][:].rearrange("p w t -> p (w t)"),
            )
            if c > 0:
                unstored = slice(0 if c == 1 else span.start, span.stop)
                nc.sync.dma_start(out_words[:, unstored], out_codes[:, unstored])

        weave_z(0)
        w2_scale = deal("w2_scale", w2_scale_raw, U8, "step3")
        multiply(0)
        weave_z(1)
        for c in range(2, CHUNKS):
            weave_z(c)
            multiply(c - 1)
        multiply(CHUNKS - 1)
        for c in range(CHUNKS):
            store_values(c)
            store_codes(c)
        for q in range(P // QUADRANT):
            nc.scalar.dma_start(
                out_2[0, PACK * q : PACK * (q + 1), :].bitcast(I32),
                out_scale[QUADRANT * q : QUADRANT * q + PACK, :].bitcast(I32),
            )
